import numpy as np
import ml_dtypes


def mxq(x, axis, fmt="e4m3"):
    dtype, down = {"e4m3": (ml_dtypes.float8_e4m3fn, 7), "e5m2": (ml_dtypes.float8_e5m2, 14)}[fmt]
    v = np.moveaxis(np.asarray(x, np.float32).astype(ml_dtypes.bfloat16).astype(np.float64), axis, -1)
    blocks = v.reshape(v.shape[:-1] + (-1, 32))
    amax = np.abs(blocks).max(-1, keepdims=True)
    byte = np.maximum(np.where(amax > 0, np.frexp(amax)[1] - 1 + 127, 0) - down, 1)
    scale = np.exp2(byte - 127.0)
    codes = (blocks / scale).astype(np.float32).astype(dtype).astype(np.float64)
    return np.moveaxis((codes * scale).reshape(v.shape), -1, axis)


WIDE = False


def mx_kscale(k):
    if not WIDE:
        return np.ones(k)
    levels = np.array([10, -10, 5, -5, 0])
    if k % 512:
        return np.exp2(np.random.permutation(np.resize(levels, k // 32))).repeat(32)
    a = np.empty((k // 512, 16))
    for p in range(k // 512):
        a[p, :8] = np.random.permutation(np.resize(levels, 8))
        for g in range(8):
            far = levels[np.abs(levels - a[p, g]) >= 10]
            a[p, g + 8] = far[np.random.randint(len(far))]
    return np.exp2(a.ravel()).repeat(32)


def f64(x):
    return np.asarray(x).astype(np.float64)


def striped(idx):
    return np.tile(idx.reshape(-1, 16).T, (8, 1)).astype(np.uint16)


def unstriped(offs):
    return offs[:16].T.reshape(-1).astype(np.int64)


E2M1 = np.array([0.0, 0.5, 1.0, 1.5, 2.0, 3.0, 4.0, 6.0, -0.0, -0.5, -1.0, -1.5, -2.0, -3.0, -4.0, -6.0])


def pack_weight(w, fmt):
    k, n = w.shape
    w = f64(np.asarray(w, np.float32).astype(ml_dtypes.bfloat16)).reshape(k // 32, 32, n)
    amax = np.abs(w).max(1)
    if fmt == "e4m3":
        byte = np.frexp(amax)[1] - 1 + 127 - 7
    else:
        mant, ex = np.frexp(amax / 6.0)
        byte = np.where(mant > 0.5, ex, ex - 1) + 127
    byte = np.clip(np.where(amax > 0, byte, 1), 1, 254)
    scaled = (w * np.exp2(127.0 - byte)[:, None, :]).reshape(k, n).astype(np.float32)
    by_word = np.ascontiguousarray(scaled.reshape(k // 512, 128, 4, n).transpose(0, 1, 3, 2))
    if fmt == "e4m3":
        words = by_word.astype(ml_dtypes.float8_e4m3fn).view(np.uint8)
    else:
        c = by_word.astype(ml_dtypes.float4_e2m1fn).view(np.uint8) & 0xF
        words = (c[..., 0::2] | (c[..., 1::2] << 4)).reshape(k // 512, 128, 2 * n)
    return np.ascontiguousarray(words), np.ascontiguousarray(byte.astype(np.uint8).reshape(k // 512, 16, n))


def unpack_weight(words, scales, fmt):
    g, _, n = scales.shape
    words = np.ascontiguousarray(words).reshape(g, 128, n, -1)
    if fmt == "e4m3":
        vals = words.view(ml_dtypes.float8_e4m3fn).astype(np.float64)
    else:
        nib = np.empty((g, 128, n, 4), np.uint8)
        nib[..., 0::2] = words & 0xF
        nib[..., 1::2] = words >> 4
        vals = E2M1[nib]
    vals = vals * np.repeat(np.exp2(scales.astype(np.float64) - 127.0), 8, axis=1)[..., None]
    return vals.transpose(0, 1, 3, 2).reshape(g * 512, n)


def silu(v):
    return v / (1.0 + np.exp(-np.maximum(v, -700.0)))


K, T, E, C, H, N = 1536, 512, 2, 256, 512, 256


def by_expert(wq, xq):
    return np.concatenate([wq[e].T @ xq[:, e * C:(e + 1) * C] for e in range(E)], axis=1)


def setup_inputs():
    n = np.random.standard_normal
    s = mx_kscale(K)[:, None]
    u = mx_kscale(H)
    w1 = [pack_weight(m, "e2m1") for m in n((E, K, H)) / np.sqrt(K) / s[None] * u[None, None, :]]
    w2 = [pack_weight(m, "e2m1") for m in n((E, H, N)) / np.sqrt(H) / u[None, :, None]]
    return {
        "xT": (n((K, T)) * s).astype(np.float32),
        "w1_words": np.stack([m[0] for m in w1]),
        "w1_scales": np.stack([m[1] for m in w1]),
        "w2_words": np.stack([m[0] for m in w2]),
        "w2_scales": np.stack([m[1] for m in w2]),
        "gate": np.tile(np.random.uniform(0.2, 1.0, E * C), (N, 1)).astype(np.float32),
        "offs": striped(np.random.permutation(T)[:E * C]),
        "dst": striped(np.random.permutation(T)[:E * C]),
    }


def reference(xT, w1_words, w1_scales, w2_words, w2_scales, gate, offs, dst):
    idx = unstriped(offs)
    w1 = np.stack([unpack_weight(w1_words[e], w1_scales[e], "e2m1") for e in range(E)])
    w2 = np.stack([unpack_weight(w2_words[e], w2_scales[e], "e2m1") for e in range(E)])
    xq = mxq(f64(xT)[:, idx], 0, "e4m3")
    h = silu(by_expert(w1, xq))
    y = by_expert(w2, mxq(h, 0, "e4m3"))
    out = np.zeros((N, T))
    out[:, unstriped(dst)] = f64(gate) * y
    return out

@@ -1,0 +1,241 @@
+from contextlib import ExitStack
+
+import concourse.mybir as mybir
+from concourse.masks import make_identity
+
+K, T, E, C, H, N = 1536, 512, 2, 256, 512, 256
+FLOPS = 2 * E * C * (K * H + H * N)
+
+F32 = mybir.dt.float32
+BF16 = mybir.dt.bfloat16
+I32 = mybir.dt.int32
+U32 = mybir.dt.uint32
+U16 = mybir.dt.uint16
+U8 = mybir.dt.uint8
+E4M3 = mybir.dt.float8_e4m3fn_x4
+E2M1 = mybir.dt.float4_e2m1fn_x4
+
+P = 128
+PASSES = K // 512
+HALF = T // 2
+COPY = mybir.ActivationFunctionType.Copy
+SILU = mybir.ActivationFunctionType.Silu
+MULT = mybir.AluOpType.mult
+
+
+def interleave_views(dst, src):
+    return (
+        dst.rearrange("p (c i) j -> p c j i", i=4),
+        src.rearrange("p j (c i) -> p c j i", i=4),
+    )
+
+
+def tile_moe_two_mlp_silu_kernel(
+    tc, xT, w1_words, w1_scales, w2_words, w2_scales, gate, offs, dst, out
+):
+    nc = tc.nc
+    with ExitStack() as ctx:
+        keep = ctx.enter_context(tc.tile_pool(name="keep", bufs=1))
+        psum = ctx.enter_context(tc.psum_pool(name="psum", bufs=1))
+
+        offs_t = keep.tile([P, T // 16], U16, name="offs_t")
+        dst_t = keep.tile([P, T // 16], U16, name="dst_t")
+        w1_sc = keep.tile([P, E * PASSES, H], U8, name="w1_sc", align_bytes=64)
+        w2_sc = keep.tile([P, E, N], U8, name="w2_sc", align_bytes=64)
+        nc.vector.memset(w1_sc[:].rearrange("p e i -> p (e i)").bitcast(I32), 0)
+        nc.vector.memset(w2_sc[:].rearrange("p e i -> p (e i)").bitcast(I32), 0)
+
+        raw = {}
+
+        def load_x(s, half):
+            rows = xT[512 * s : 512 * (s + 1), :].rearrange("(p j) t -> p j t", j=4)
+            tile = keep.tile([P, 4, HALF], F32, name=f"raw{s}_{half}")
+            nc.sync.dma_start(tile[:], rows[:, :, HALF * half : HALF * (half + 1)])
+            raw[s, half] = tile
+
+        w1_t = {}
+
+        def load_w1(e, s0, s1):
+            tile = keep.tile([P, s1 - s0, 2 * H], U8, name=f"w1_{e}_{s0}", align_bytes=64)
+            nc.sync.dma_start(tile[:], w1_words[e, s0:s1].rearrange("s p c -> p s c"))
+            for s in range(s0, s1):
+                w1_t[e, s] = tile[:, s - s0, :]
+
+        load_x(0, 0)
+        load_x(0, 1)
+        nc.sync.dma_start(offs_t[:], offs)
+        load_x(1, 0)
+        load_x(1, 1)
+        load_w1(0, 0, 2)
+        for q in range(4):
+            nc.sync.dma_start(
+                w1_sc[32 * q : 32 * q + 4].bitcast(I32),
+                w1_scales[:, :, 4 * q : 4 * q + 4, :].rearrange("e s q i -> q (e s) i").bitcast(I32),
+            )
+        load_x(2, 0)
+        load_x(2, 1)
+        load_w1(0, 2, 3)
+        load_w1(1, 0, 3)
+        w2_t = keep.tile([P, E, 2 * N], U8, name="w2_t", align_bytes=64)
+        gate_t = keep.tile([P, 2, T], F32, name="gate_t")
+
+        for q in range(4):
+            nc.sync.dma_start(
+                w2_sc[32 * q : 32 * q + 4].bitcast(I32),
+                w2_scales[:, 0, 4 * q : 4 * q + 4, :].rearrange("e q n -> q e n").bitcast(I32),
+            )
+        nc.sync.dma_start(w2_t[:], w2_words.rearrange("e s p c -> p (e s) c"))
+        nc.sync.dma_start(dst_t[:], dst)
+        nc.sync.dma_start(gate_t[:], gate.rearrange("(h p) j -> p h j", h=2))
+
+        ident = keep.tile([P, P], F32, name="ident")
+        make_identity(nc, ident[:])
+        warm = keep.tile([P, 1], F32, name="warm")
+        nc.gpsimd.memset(warm[:], 0.0)
+        warm_out = keep.tile([P, 1], F32, name="warm_out")
+        nc.scalar.activation(warm_out[:], warm[:], SILU)
+
+        scales = [keep.tile([P, T], U8, name=f"scales{s}", align_bytes=64) for s in range(PASSES)]
+        for s in range(PASSES):
+            nc.gpsimd.memset(scales[s][:], 0)
+
+        acc = [psum.tile([P, H], F32, name=f"acc{b}") for b in range(4)]
+        turned = [psum.tile([P, 2, P], F32, name=f"turned{b}") for b in range(2)]
+        y = [psum.tile([P, 2, C], F32, name=f"y{i}") for i in range(2)]
+
+        words = [keep.tile([P, T], U32, name=f"words{s}", align_bytes=64) for s in range(PASSES)]
+        gw = {}
+        gs = {}
+
+        def quantise(s, half, vector_from):
+            parts = [(nc.scalar, 0, vector_from), (nc.vector, vector_from, HALF)]
+            for engine, t0, t1 in parts:
+                if t0 == t1:
+                    continue
+                grouped = keep.tile([P, t1 - t0, 4], BF16, name=f"grouped{s}_{half}_{t0}", align_bytes=64)
+                to, frm = interleave_views(grouped[:], raw[s, half][:, :, t0:t1])
+                if engine is nc.scalar:
+                    nc.scalar.activation(to, frm, COPY)
+                else:
+                    nc.vector.tensor_copy(to, frm)
+                cols = slice(HALF * half + t0, HALF * half + t1)
+                nc.vector.quantize_mx(
+                    out=words[s][:, cols].bitcast(E4M3),
+                    scales=scales[s][:, cols],
+                    in_=grouped[:].rearrange("p t j -> p (t j)"),
+                )
+
+        def gather(s, c0, c1):
+            w = keep.tile([P, c1 - c0], U32, name=f"gw{s}_{c0}", align_bytes=64)
+            nc.vector.tensor_copy(w[:], words[s][:].indirect(offs_t[:, c0 // 16 : c1 // 16]))
+            g = keep.tile([P, c1 - c0], U8, name=f"gs{s}_{c0}", align_bytes=64)
+            nc.vector.tensor_copy(g[:], scales[s][:].indirect(offs_t[:, c0 // 16 : c1 // 16]))
+            for b in range(c0 // P, c1 // P):
+                gw[s, b] = w[:, P * b - c0 : P * b - c0 + P]
+                gs[s, b] = g[:, P * b - c0 : P * b - c0 + P]
+
+        def first_layer(s, b):
+            e = b // 2
+            nc.tensor.matmul_mx(
+                out=acc[b][:],
+                lhsT=gw[s, b].bitcast(E4M3),
+                lhsT_scale=gs[s, b],
+                rhs=w1_t[e, s].bitcast(E2M1),
+                rhs_scale=w1_sc[:, e * PASSES + s, :],
+                start=(s == 0),
+                stop=(s == PASSES - 1),
+            )
+
+        h_t = {}
+
+        def activate(b):
+            h = keep.tile([P, H], BF16, name=f"h{b}")
+            nc.scalar.activation(h[:], acc[b][:], SILU)
+            h_t[b] = h
+
+        def turn(b):
+            h_pairs = h_t[b][:].bitcast(F32)
+            for u in range(2):
+                nc.tensor.transpose(turned[b % 2][:, u, :], h_pairs[:, u::2], ident[:])
+
+        grouped_h = {}
+
+        def regroup(b, c0, c1):
+            if c0 not in grouped_h:
+                grouped_h[c0] = keep.tile([P, c1 - c0, 4], BF16, name=f"hgrouped{c0}", align_bytes=64)
+            pairs = grouped_h[c0][:].rearrange("p r f -> p (r f)").bitcast(F32).rearrange("p (r u) -> p r u", u=2)
+            nc.scalar.copy(pairs[:, P * b - c0 : P * b - c0 + P, :], turned[b % 2][:].rearrange("p u r -> p r u"))
+
+        windows = [keep.tile([P, T], F32, name=f"window{nh}") for nh in range(2)]
+        ysb = {}
+
+        def second_layer(c0, c1, bank):
+            e, n = c0 // C, c1 - c0
+            hw = keep.tile([P, n], U32, name=f"hw{c0}", align_bytes=64)
+            hsc = keep.tile([P, n], U8, name=f"hsc{c0}", align_bytes=64)
+            nc.vector.quantize_mx(
+                out=hw[:].bitcast(E4M3), scales=hsc[:], in_=grouped_h[c0][:].rearrange("p r f -> p (r f)")
+            )
+            for nh in range(2):
+                nc.tensor.matmul_mx(
+                    out=y[bank][:, nh, 0:n],
+                    lhsT=w2_t[:, e, N * nh : N * (nh + 1)].bitcast(E2M1),
+                    lhsT_scale=w2_sc[:, e, P * nh : P * (nh + 1)],
+                    rhs=hw[:].bitcast(E4M3),
+                    rhs_scale=hsc[:],
+                    start=True,
+                    stop=True,
+                )
+            for nh in range(2):
+                yt = keep.tile([P, n], F32, name=f"ysb{c0}_{nh}")
+                nc.scalar.activation(yt[:], y[bank][:, nh, 0:n], COPY)
+                ysb[c0, nh] = yt
+
+        def scatter(c0, c1):
+            for nh in range(2):
+                nc.vector.tensor_tensor(
+                    windows[nh][:].indirect(dst_t[:, c0 // 16 : c1 // 16]),
+                    ysb[c0, nh][:],
+                    gate_t[:, nh, c0:c1],
+                    MULT,
+                )
+
+        quantise(0, 0, 0)
+        quantise(0, 1, P)
+        gather(0, 0, C)
+        first_layer(0, 0)
+        first_layer(0, 1)
+        gather(0, C, T)
+        quantise(1, 0, HALF)
+        quantise(1, 1, HALF)
+        gather(1, 0, C)
+        first_layer(1, 0)
+        first_layer(1, 1)
+        quantise(2, 0, HALF)
+        quantise(2, 1, P)
+        for b in range(2):
+            gather(2, P * b, P * (b + 1))
+            first_layer(2, b)
+            activate(b)
+            turn(b)
+            regroup(b, P * b, P * (b + 1))
+        gather(1, C, T)
+        first_layer(0, 2)
+        first_layer(0, 3)
+        first_layer(1, 2)
+        first_layer(1, 3)
+        second_layer(0, P, 0)
+        gather(2, C, T)
+        second_layer(P, C, 1)
+        first_layer(2, 2)
+        first_layer(2, 3)
+        scatter(0, P)
+        for b in range(2, 4):
+            activate(b)
+            turn(b)
+            regroup(b, C, T)
+        scatter(P, C)
+        second_layer(C, T, 0)
+        scatter(C, T)
+        for nh in range(2):
+            nc.sync.dma_start(out[P * nh : P * (nh + 1), :], windows[nh][:])

@@ -55,27 +55,28 @@ def tile_moe_two_mlp_silu_kernel(
 
         w1_t = {}
 
-        def load_w1(e, s0, s1):
-            tile = keep.tile([P, s1 - s0, 2 * H], U8, name=f"w1_{e}_{s0}", align_bytes=64)
-            nc.sync.dma_start(tile[:], w1_words[e, s0:s1].rearrange("s p c -> p s c"))
-            for s in range(s0, s1):
-                w1_t[e, s] = tile[:, s - s0, :]
+        def load_w1(s0, s1):
+            n = s1 - s0
+            tile = keep.tile([P, E * n, 2 * H], U8, name=f"w1_{s0}", align_bytes=64)
+            for e in range(E):
+                nc.sync.dma_start(tile[:, n * e : n * (e + 1), :], w1_words[e, s0:s1].rearrange("s p c -> p s c"))
+                for s in range(s0, s1):
+                    w1_t[e, s] = tile[:, n * e + s - s0, :]
 
         load_x(0, 0)
         load_x(0, 1)
         nc.sync.dma_start(offs_t[:], offs)
         load_x(1, 0)
         load_x(1, 1)
-        load_w1(0, 0, 2)
         for q in range(4):
             nc.sync.dma_start(
                 w1_sc[32 * q : 32 * q + 4].bitcast(I32),
                 w1_scales[:, :, 4 * q : 4 * q + 4, :].rearrange("e s q i -> q (e s) i").bitcast(I32),
             )
+        load_w1(0, 1)
         load_x(2, 0)
         load_x(2, 1)
-        load_w1(0, 2, 3)
-        load_w1(1, 0, 3)
+        load_w1(1, 3)
         w2_t = keep.tile([P, E, 2 * N], U8, name="w2_t", align_bytes=64)
         gate_t = keep.tile([P, 2, T], F32, name="gate_t")
 
@@ -200,32 +201,28 @@ def tile_moe_two_mlp_silu_kernel(
                     MULT,
                 )
 
-        quantise(0, 0, 0)
+        quantise(0, 0, P)
         quantise(0, 1, P)
-        gather(0, 0, C)
-        first_layer(0, 0)
-        first_layer(0, 1)
-        gather(0, C, T)
+        for e in range(E):
+            gather(0, C * e, C * (e + 1))
+        for b in range(4):
+            first_layer(0, b)
         quantise(1, 0, HALF)
         quantise(1, 1, HALF)
-        gather(1, 0, C)
-        first_layer(1, 0)
-        first_layer(1, 1)
+        for e in range(E):
+            gather(1, C * e, C * (e + 1))
+        for b in range(4):
+            first_layer(1, b)
         quantise(2, 0, HALF)
-        quantise(2, 1, P)
+        quantise(2, 1, HALF)
         for b in range(2):
             gather(2, P * b, P * (b + 1))
             first_layer(2, b)
             activate(b)
             turn(b)
             regroup(b, P * b, P * (b + 1))
-        gather(1, C, T)
-        first_layer(0, 2)
-        first_layer(0, 3)
-        first_layer(1, 2)
-        first_layer(1, 3)
-        second_layer(0, P, 0)
         gather(2, C, T)
+        second_layer(0, P, 0)
         second_layer(P, C, 1)
         first_layer(2, 2)
         first_layer(2, 3)
@@ -234,8 +231,8 @@ def tile_moe_two_mlp_silu_kernel(
             activate(b)
             turn(b)
             regroup(b, C, T)
-        scatter(P, C)
         second_layer(C, T, 0)
+        scatter(P, C)
         scatter(C, T)
         for nh in range(2):
             nc.sync.dma_start(out[P * nh : P * (nh + 1), :], windows[nh][:])

@@ -45,6 +45,10 @@ def tile_moe_two_mlp_silu_kernel(
         nc.vector.memset(w1_sc[:].rearrange("p e i -> p (e i)").bitcast(I32), 0)
         nc.vector.memset(w2_sc[:].rearrange("p e i -> p (e i)").bitcast(I32), 0)
 
+        scales = [keep.tile([P, T], U8, name=f"scales{s}", align_bytes=64) for s in range(PASSES)]
+        for s in range(PASSES):
+            nc.gpsimd.memset(scales[s][:].bitcast(I32), 0)
+
         raw = {}
 
         def load_x(s, half):
@@ -55,13 +59,11 @@ def tile_moe_two_mlp_silu_kernel(
 
         w1_t = {}
 
-        def load_w1(s0, s1):
-            n = s1 - s0
-            tile = keep.tile([P, E * n, 2 * H], U8, name=f"w1_{s0}", align_bytes=64)
+        def load_w1(s):
+            tile = keep.tile([P, E, 2 * H], U8, name=f"w1_{s}", align_bytes=64)
+            nc.sync.dma_start(tile[:], w1_words[:, s].rearrange("e p c -> p e c"))
             for e in range(E):
-                nc.sync.dma_start(tile[:, n * e : n * (e + 1), :], w1_words[e, s0:s1].rearrange("s p c -> p s c"))
-                for s in range(s0, s1):
-                    w1_t[e, s] = tile[:, n * e + s - s0, :]
+                w1_t[e, s] = tile[:, e, :]
 
         load_x(0, 0)
         load_x(0, 1)
@@ -73,10 +75,11 @@ def tile_moe_two_mlp_silu_kernel(
                 w1_sc[32 * q : 32 * q + 4].bitcast(I32),
                 w1_scales[:, :, 4 * q : 4 * q + 4, :].rearrange("e s q i -> q (e s) i").bitcast(I32),
             )
-        load_w1(0, 1)
+        load_w1(0)
         load_x(2, 0)
         load_x(2, 1)
-        load_w1(1, 3)
+        load_w1(1)
+        load_w1(2)
         w2_t = keep.tile([P, E, 2 * N], U8, name="w2_t", align_bytes=64)
         gate_t = keep.tile([P, 2, T], F32, name="gate_t")
 
@@ -96,9 +99,6 @@ def tile_moe_two_mlp_silu_kernel(
         warm_out = keep.tile([P, 1], F32, name="warm_out")
         nc.scalar.activation(warm_out[:], warm[:], SILU)
 
-        scales = [keep.tile([P, T], U8, name=f"scales{s}", align_bytes=64) for s in range(PASSES)]
-        for s in range(PASSES):
-            nc.gpsimd.memset(scales[s][:], 0)
 
         acc = [psum.tile([P, H], F32, name=f"acc{b}") for b in range(4)]
         turned = [psum.tile([P, 2, P], F32, name=f"turned{b}") for b in range(2)]

@@ -113,7 +113,7 @@ def tile_moe_two_mlp_silu_kernel(
             for engine, t0, t1 in parts:
                 if t0 == t1:
                     continue
-                grouped = keep.tile([P, t1 - t0, 4], BF16, name=f"grouped{s}_{half}_{t0}", align_bytes=64)
+                grouped = keep.tile([P, t1 - t0, 4], BF16, name=f"grouped{s}_{half}_{t0}", tag=f"grouped{s}_{half}_{t0}", align_bytes=64)
                 to, frm = interleave_views(grouped[:], raw[s, half][:, :, t0:t1])
                 if engine is nc.scalar:
                     nc.scalar.activation(to, frm, COPY)
@@ -126,13 +126,17 @@ def tile_moe_two_mlp_silu_kernel(
                     in_=grouped[:].rearrange("p t j -> p (t j)"),
                 )
 
-        def gather(s, c0, c1):
+        def gather_words(s, c0, c1):
             w = keep.tile([P, c1 - c0], U32, name=f"gw{s}_{c0}", align_bytes=64)
             nc.vector.tensor_copy(w[:], words[s][:].indirect(offs_t[:, c0 // 16 : c1 // 16]))
-            g = keep.tile([P, c1 - c0], U8, name=f"gs{s}_{c0}", align_bytes=64)
-            nc.vector.tensor_copy(g[:], scales[s][:].indirect(offs_t[:, c0 // 16 : c1 // 16]))
             for b in range(c0 // P, c1 // P):
                 gw[s, b] = w[:, P * b - c0 : P * b - c0 + P]
+
+        def gather_scales(s, c0, c1, tag=None):
+            name = f"gs{s}_{c0}"
+            g = keep.tile([P, c1 - c0], U8, name=name, tag=name if tag is None else tag, align_bytes=64)
+            nc.vector.tensor_copy(g[:], scales[s][:].indirect(offs_t[:, c0 // 16 : c1 // 16]))
+            for b in range(c0 // P, c1 // P):
                 gs[s, b] = g[:, P * b - c0 : P * b - c0 + P]
 
         def first_layer(s, b):
@@ -203,25 +207,35 @@ def tile_moe_two_mlp_silu_kernel(
 
         quantise(0, 0, P)
         quantise(0, 1, P)
-        for e in range(E):
-            gather(0, C * e, C * (e + 1))
-        for b in range(4):
+        gather_words(0, 0, C)
+        gather_scales(0, 0, C)
+        for b in range(2):
             first_layer(0, b)
+        gather_words(0, C, T)
         quantise(1, 0, HALF)
         quantise(1, 1, HALF)
-        for e in range(E):
-            gather(1, C * e, C * (e + 1))
-        for b in range(4):
+        gather_scales(0, C, T, tag="grouped1_0_0")
+        for b in range(2, 4):
+            first_layer(0, b)
+        gather_words(1, 0, C)
+        gather_scales(1, 0, C)
+        for b in range(2):
             first_layer(1, b)
+        gather_words(1, C, T)
         quantise(2, 0, HALF)
         quantise(2, 1, HALF)
+        gather_scales(1, C, T, tag="grouped2_0_0")
+        for b in range(2, 4):
+            first_layer(1, b)
         for b in range(2):
-            gather(2, P * b, P * (b + 1))
+            gather_words(2, P * b, P * (b + 1))
+            gather_scales(2, P * b, P * (b + 1))
             first_layer(2, b)
             activate(b)
             turn(b)
             regroup(b, P * b, P * (b + 1))
-        gather(2, C, T)
+        gather_words(2, C, T)
+        gather_scales(2, C, T)
         second_layer(0, P, 0)
         second_layer(P, C, 1)
         first_layer(2, 2)

from contextlib import ExitStack

import concourse.mybir as mybir
from concourse.masks import make_identity

K, T, E, C, H, N = 1536, 512, 2, 256, 512, 256
FLOPS = 2 * E * C * (K * H + H * N)

F32 = mybir.dt.float32
BF16 = mybir.dt.bfloat16
I32 = mybir.dt.int32
U32 = mybir.dt.uint32
U16 = mybir.dt.uint16
U8 = mybir.dt.uint8
E4M3 = mybir.dt.float8_e4m3fn_x4
E2M1 = mybir.dt.float4_e2m1fn_x4

P = 128
PASSES = K // 512
HALF = T // 2
COPY = mybir.ActivationFunctionType.Copy
SILU = mybir.ActivationFunctionType.Silu
MULT = mybir.AluOpType.mult


def interleave_views(dst, src):
    return (
        dst.rearrange("p (c i) j -> p c j i", i=4),
        src.rearrange("p j (c i) -> p c j i", i=4),
    )


def tile_moe_two_mlp_silu_kernel(
    tc, xT, w1_words, w1_scales, w2_words, w2_scales, gate, offs, dst, out
):
    nc = tc.nc
    with ExitStack() as ctx:
        keep = ctx.enter_context(tc.tile_pool(name="keep", bufs=1))
        psum = ctx.enter_context(tc.psum_pool(name="psum", bufs=1))

        offs_t = keep.tile([P, T // 16], U16, name="offs_t")
        dst_t = keep.tile([P, T // 16], U16, name="dst_t")
        w1_sc = keep.tile([P, E * PASSES, H], U8, name="w1_sc", align_bytes=64)
        w2_sc = keep.tile([P, E, N], U8, name="w2_sc", align_bytes=64)
        nc.vector.memset(w1_sc[:].rearrange("p e i -> p (e i)").bitcast(I32), 0)
        nc.vector.memset(w2_sc[:].rearrange("p e i -> p (e i)").bitcast(I32), 0)

        scales = [keep.tile([P, T], U8, name=f"scales{s}", align_bytes=64) for s in range(PASSES)]
        for s in range(PASSES):
            nc.gpsimd.memset(scales[s][:].bitcast(I32), 0)

        raw = {}

        def load_x(s, half):
            rows = xT[512 * s : 512 * (s + 1), :].rearrange("(p j) t -> p j t", j=4)
            tile = keep.tile([P, 4, HALF], F32, name=f"raw{s}_{half}")
            nc.sync.dma_start(tile[:], rows[:, :, HALF * half : HALF * (half + 1)])
            raw[s, half] = tile

        w1_t = {}

        def load_w1(s):
            tile = keep.tile([P, E, 2 * H], U8, name=f"w1_{s}", align_bytes=64)
            nc.sync.dma_start(tile[:], w1_words[:, s].rearrange("e p c -> p e c"))
            for e in range(E):
                w1_t[e, s] = tile[:, e, :]

        load_x(0, 0)
        load_x(0, 1)
        nc.sync.dma_start(offs_t[:], offs)
        load_x(1, 0)
        load_x(1, 1)
        for q in range(4):
            nc.sync.dma_start(
                w1_sc[32 * q : 32 * q + 4].bitcast(I32),
                w1_scales[:, :, 4 * q : 4 * q + 4, :].rearrange("e s q i -> q (e s) i").bitcast(I32),
            )
        load_w1(0)
        load_x(2, 0)
        load_x(2, 1)
        load_w1(1)
        load_w1(2)
        w2_t = keep.tile([P, E, 2 * N], U8, name="w2_t", align_bytes=64)
        gate_t = keep.tile([P, 2, T], F32, name="gate_t")

        for q in range(4):
            nc.sync.dma_start(
                w2_sc[32 * q : 32 * q + 4].bitcast(I32),
                w2_scales[:, 0, 4 * q : 4 * q + 4, :].rearrange("e q n -> q e n").bitcast(I32),
            )
        nc.sync.dma_start(w2_t[:], w2_words.rearrange("e s p c -> p (e s) c"))
        nc.sync.dma_start(dst_t[:], dst)
        nc.sync.dma_start(gate_t[:], gate.rearrange("(h p) j -> p h j", h=2))

        ident = keep.tile([P, P], F32, name="ident")
        make_identity(nc, ident[:])
        warm = keep.tile([P, 1], F32, name="warm")
        nc.gpsimd.memset(warm[:], 0.0)
        warm_out = keep.tile([P, 1], F32, name="warm_out")
        nc.scalar.activation(warm_out[:], warm[:], SILU)


        acc = [psum.tile([P, H], F32, name=f"acc{b}") for b in range(4)]
        turned = [psum.tile([P, 2, P], F32, name=f"turned{b}") for b in range(2)]
        y = [psum.tile([P, 2, C], F32, name=f"y{i}") for i in range(2)]

        words = [keep.tile([P, T], U32, name=f"words{s}", align_bytes=64) for s in range(PASSES)]
        gw = {}
        gs = {}

        def quantise(s, half, vector_from):
            parts = [(nc.scalar, 0, vector_from), (nc.vector, vector_from, HALF)]
            for engine, t0, t1 in parts:
                if t0 == t1:
                    continue
                grouped = keep.tile([P, t1 - t0, 4], BF16, name=f"grouped{s}_{half}_{t0}", tag=f"grouped{s}_{half}_{t0}", align_bytes=64)
                to, frm = interleave_views(grouped[:], raw[s, half][:, :, t0:t1])
                if engine is nc.scalar:
                    nc.scalar.activation(to, frm, COPY)
                else:
                    nc.vector.tensor_copy(to, frm)
                cols = slice(HALF * half + t0, HALF * half + t1)
                nc.vector.quantize_mx(
                    out=words[s][:, cols].bitcast(E4M3),
                    scales=scales[s][:, cols],
                    in_=grouped[:].rearrange("p t j -> p (t j)"),
                )

        def gather_words(s, c0, c1):
            w = keep.tile([P, c1 - c0], U32, name=f"gw{s}_{c0}", align_bytes=64)
            nc.vector.tensor_copy(w[:], words[s][:].indirect(offs_t[:, c0 // 16 : c1 // 16]))
            for b in range(c0 // P, c1 // P):
                gw[s, b] = w[:, P * b - c0 : P * b - c0 + P]

        def gather_scales(s, c0, c1, tag=None):
            name = f"gs{s}_{c0}"
            g = keep.tile([P, c1 - c0], U8, name=name, tag=name if tag is None else tag, align_bytes=64)
            nc.vector.tensor_copy(g[:], scales[s][:].indirect(offs_t[:, c0 // 16 : c1 // 16]))
            for b in range(c0 // P, c1 // P):
                gs[s, b] = g[:, P * b - c0 : P * b - c0 + P]

        def first_layer(s, b):
            e = b // 2
            nc.tensor.matmul_mx(
                out=acc[b][:],
                lhsT=gw[s, b].bitcast(E4M3),
                lhsT_scale=gs[s, b],
                rhs=w1_t[e, s].bitcast(E2M1),
                rhs_scale=w1_sc[:, e * PASSES + s, :],
                start=(s == 0),
                stop=(s == PASSES - 1),
            )

        h_t = {}

        def activate(b):
            h = keep.tile([P, H], BF16, name=f"h{b}")
            nc.scalar.activation(h[:], acc[b][:], SILU)
            h_t[b] = h

        def turn(b):
            h_pairs = h_t[b][:].bitcast(F32)
            for u in range(2):
                nc.tensor.transpose(turned[b % 2][:, u, :], h_pairs[:, u::2], ident[:])

        grouped_h = {}

        def regroup(b, c0, c1):
            if c0 not in grouped_h:
                grouped_h[c0] = keep.tile([P, c1 - c0, 4], BF16, name=f"hgrouped{c0}", align_bytes=64)
            pairs = grouped_h[c0][:].rearrange("p r f -> p (r f)").bitcast(F32).rearrange("p (r u) -> p r u", u=2)
            nc.scalar.copy(pairs[:, P * b - c0 : P * b - c0 + P, :], turned[b % 2][:].rearrange("p u r -> p r u"))

        windows = [keep.tile([P, T], F32, name=f"window{nh}") for nh in range(2)]
        ysb = {}

        def second_layer(c0, c1, bank):
            e, n = c0 // C, c1 - c0
            hw = keep.tile([P, n], U32, name=f"hw{c0}", align_bytes=64)
            hsc = keep.tile([P, n], U8, name=f"hsc{c0}", align_bytes=64)
            nc.vector.quantize_mx(
                out=hw[:].bitcast(E4M3), scales=hsc[:], in_=grouped_h[c0][:].rearrange("p r f -> p (r f)")
            )
            for nh in range(2):
                nc.tensor.matmul_mx(
                    out=y[bank][:, nh, 0:n],
                    lhsT=w2_t[:, e, N * nh : N * (nh + 1)].bitcast(E2M1),
                    lhsT_scale=w2_sc[:, e, P * nh : P * (nh + 1)],
                    rhs=hw[:].bitcast(E4M3),
                    rhs_scale=hsc[:],
                    start=True,
                    stop=True,
                )
            for nh in range(2):
                yt = keep.tile([P, n], F32, name=f"ysb{c0}_{nh}")
                nc.scalar.activation(yt[:], y[bank][:, nh, 0:n], COPY)
                ysb[c0, nh] = yt

        def scatter(c0, c1):
            for nh in range(2):
                nc.vector.tensor_tensor(
                    windows[nh][:].indirect(dst_t[:, c0 // 16 : c1 // 16]),
                    ysb[c0, nh][:],
                    gate_t[:, nh, c0:c1],
                    MULT,
                )

        quantise(0, 0, P)
        quantise(0, 1, P)
        gather_words(0, 0, C)
        gather_scales(0, 0, C)
        for b in range(2):
            first_layer(0, b)
        gather_words(0, C, T)
        quantise(1, 0, HALF)
        quantise(1, 1, HALF)
        gather_scales(0, C, T, tag="grouped1_0_0")
        for b in range(2, 4):
            first_layer(0, b)
        gather_words(1, 0, C)
        gather_scales(1, 0, C)
        for b in range(2):
            first_layer(1, b)
        gather_words(1, C, T)
        quantise(2, 0, HALF)
        quantise(2, 1, HALF)
        gather_scales(1, C, T, tag="grouped2_0_0")
        for b in range(2, 4):
            first_layer(1, b)
        for b in range(2):
            gather_words(2, P * b, P * (b + 1))
            gather_scales(2, P * b, P * (b + 1))
            first_layer(2, b)
            activate(b)
            turn(b)
            regroup(b, P * b, P * (b + 1))
        gather_words(2, C, T)
        gather_scales(2, C, T)
        second_layer(0, P, 0)
        second_layer(P, C, 1)
        first_layer(2, 2)
        first_layer(2, 3)
        scatter(0, P)
        for b in range(2, 4):
            activate(b)
            turn(b)
            regroup(b, C, T)
        second_layer(C, T, 0)
        scatter(P, C)
        scatter(C, T)
        for nh in range(2):
            nc.sync.dma_start(out[P * nh : P * (nh + 1), :], windows[nh][:])
